import numpy as np
CORES = [7,135,263,391,15,143,271,399,23,151,279,407,31,159,287,415]
N = 16
def setup_inputs(rng):
    return {"x": rng.standard_normal((N, 128, 256), dtype=np.float32)}
def reference(x):
    s = np.cumsum(x.astype(np.float64), axis=0)
    return {"y": s.astype(x.dtype)}

@@ -1,0 +1,78 @@
+from concourse.bass import DstId, RemoteDMATransfer
+from concourse.mybir import AluOpType
+
+W = 256
+SCRATCH = {
+    "xs": ("dram", [128, W], "float32"),
+    "xp": ("dram", [128, W], "float32"),
+    "pc": ("dram", [3, 128, W], "float32"),
+    "cb": ("dram", [128, W], "float32"),
+}
+SEMAPHORES = ["ld", "yc", "r1", "r2", "r3", "sent", "acc"]
+OFF = 0x00FF
+
+
+def rank_program(g, core, T, topo):
+    rank = T.rank_of(core)
+    if rank is None:
+        return
+    c, h = rank // 4, rank % 4
+    S = T.sem
+
+    def at(cc, hh):
+        return T.cores[4 * cc + hh]
+
+    def send(srcs, dst_ap, dsts, sem):
+        ids = []
+        for d in dsts:
+            rid, pid = topo.addr(d, core)
+            ids.append(DstId(rid=rid, pnc=pid))
+        g.remote_dma_fused(
+            [RemoteDMATransfer(dst_ids=ids, dma_engine_mask=OFF, remote_sem=sem, srcs=srcs,
+                               dsts=[dst_ap for _ in dsts], alu_op=1 if len(srcs) > 1 else 0)],
+            local_sem=S.sent)
+        sent[0] += 8
+
+    sent = [0]
+    nacc = [0]
+
+    def add(src):
+        if nacc[0]:
+            g.wait_ge(S.acc, 16 * nacc[0])
+        g.dma_start(T.y[:], src, accum_op=AluOpType.add).then_inc(S.acc, 16)
+        nacc[0] += 1
+
+    high = h % 2 == 1
+    rack1 = h >= 2
+    g.sync.dma_start(T.xs[:], T.x[:]).then_inc(S.ld, 16)
+    g.scalar.dma_start(T.y[:], T.x[:]).then_inc(S.yc, 16)
+
+    g.wait_ge(S.ld, 16)
+    if not (c == 3 and h == 3):
+        send([T.xs[:]], T.xp[:], [at(c, h ^ 1)], S.r1)
+    got_xp = not (c == 3 and h == 2)
+    if got_xp:
+        g.wait_ge(S.r1, 8)
+
+    if c < 3:
+        send([T.xs[:], T.xp[:]], T.pc[c], [at(cc, h) for cc in range(c + 1, 4)], S.r2)
+    g.wait_ge(S.yc, 16)
+    if high:
+        add(T.xp[:])
+    if c:
+        g.wait_ge(S.r2, 8 * c)
+
+    below = [T.pc[k] for k in range(c)]
+    if not rack1:
+        send([T.xs[:], T.xp[:]] + below, T.cb[:], [at(c, h ^ 3)], S.r3)
+    elif c:
+        send(below, T.cb[:], [at(c, h ^ 3)], S.r3)
+    for b in below:
+        add(b)
+    if rack1 or c:
+        g.wait_ge(S.r3, 8)
+        add(T.cb[:])
+    if nacc[0]:
+        g.wait_ge(S.acc, 16 * nacc[0])
+    if sent[0]:
+        g.wait_ge(S.sent, sent[0])

@@ -1,78 +1,92 @@
 from concourse.bass import DstId, RemoteDMATransfer
-from concourse.mybir import AluOpType
 
-W = 256
-SCRATCH = {
-    "xs": ("dram", [128, W], "float32"),
-    "xp": ("dram", [128, W], "float32"),
-    "pc": ("dram", [3, 128, W], "float32"),
-    "cb": ("dram", [128, W], "float32"),
-}
-SEMAPHORES = ["ld", "yc", "r1", "r2", "r3", "sent", "acc"]
-OFF = 0x00FF
+COLLECTOR = 3
+HALF_OF_HOST = (0, 1, 1, 0)
+SCRATCH = {"buf": ("dram", [9, 128, 128], "float32")}
+XS, FIN, CB = 0, 2, 8
+SEMAPHORES = ["ld", "r1", "r2", "f0", "f1", "st", "sent"]
+LO4, HI4, OFF8, ON8 = 0x000F, 0x00F0, 0x00FF, 0xFF00
+
+
+def bits(m):
+    return sum((m >> i) & 1 for i in range(16))
+
+
+def world(c, h, k):
+    return 128 * h + 8 * c + k
+
+
+def write1_plan(c, h):
+    plan = []
+    for hh in (h & 2, (h & 2) + 1):
+        k = HALF_OF_HOST[hh]
+        far = [(cc, hh) for cc in range(c, 4) if (cc, hh) != (c, h)]
+        if hh == h:
+            plan.append((k, ON8, [(c, h)]))
+            if far:
+                plan.append((k, LO4, far))
+        else:
+            plan.append((k, HI4 if c < 3 else OFF8, far))
+    return plan
 
 
 def rank_program(g, core, T, topo):
-    rank = T.rank_of(core)
-    if rank is None:
-        return
-    c, h = rank // 4, rank % 4
     S = T.sem
+    buf = T.buf
+    h, c, k = topo.host(core), topo.chip(core), core % 8
+    if c > 3 or k not in (7, COLLECTOR):
+        return
+    sent = [0]
 
-    def at(cc, hh):
-        return T.cores[4 * cc + hh]
-
-    def send(srcs, dst_ap, dsts, sem):
+    def transfer(srcs, slot, dsts, mask, sem):
         ids = []
         for d in dsts:
             rid, pid = topo.addr(d, core)
             ids.append(DstId(rid=rid, pnc=pid))
+        sent[0] += bits(mask)
+        return RemoteDMATransfer(dst_ids=ids, dma_engine_mask=mask, remote_sem=sem, srcs=[buf[s] for s in srcs],
+                                 dsts=[buf[slot] for _ in dsts], alu_op=1 if len(srcs) > 1 else 0)
+
+    if k == 7:
+        g.sync.dma_start(buf[XS:XS + 2], T.x[:]).then_inc(S.ld, 16)
+        if (c, h) == (0, 0):
+            g.scalar.dma_start(T.y[:], T.x[:]).then_inc(S.st, 16)
+        g.wait_ge(S.ld, 16)
+        slot = 2 * c + h % 2
         g.remote_dma_fused(
-            [RemoteDMATransfer(dst_ids=ids, dma_engine_mask=OFF, remote_sem=sem, srcs=srcs,
-                               dsts=[dst_ap for _ in dsts], alu_op=1 if len(srcs) > 1 else 0)],
-            local_sem=S.sent)
-        sent[0] += 8
-
-    sent = [0]
-    nacc = [0]
-
-    def add(src):
-        if nacc[0]:
-            g.wait_ge(S.acc, 16 * nacc[0])
-        g.dma_start(T.y[:], src, accum_op=AluOpType.add).then_inc(S.acc, 16)
-        nacc[0] += 1
-
-    high = h % 2 == 1
-    rack1 = h >= 2
-    g.sync.dma_start(T.xs[:], T.x[:]).then_inc(S.ld, 16)
-    g.scalar.dma_start(T.y[:], T.x[:]).then_inc(S.yc, 16)
-
-    g.wait_ge(S.ld, 16)
-    if not (c == 3 and h == 3):
-        send([T.xs[:]], T.xp[:], [at(c, h ^ 1)], S.r1)
-    got_xp = not (c == 3 and h == 2)
-    if got_xp:
-        g.wait_ge(S.r1, 8)
-
-    if c < 3:
-        send([T.xs[:], T.xp[:]], T.pc[c], [at(cc, h) for cc in range(c + 1, 4)], S.r2)
-    g.wait_ge(S.yc, 16)
-    if high:
-        add(T.xp[:])
-    if c:
-        g.wait_ge(S.r2, 8 * c)
-
-    below = [T.pc[k] for k in range(c)]
-    if not rack1:
-        send([T.xs[:], T.xp[:]] + below, T.cb[:], [at(c, h ^ 3)], S.r3)
-    elif c:
-        send(below, T.cb[:], [at(c, h ^ 3)], S.r3)
-    for b in below:
-        add(b)
-    if rack1 or c:
-        g.wait_ge(S.r3, 8)
-        add(T.cb[:])
-    if nacc[0]:
-        g.wait_ge(S.acc, 16 * nacc[0])
-    if sent[0]:
+            [transfer([XS + half], slot, [world(cc, hh, COLLECTOR) for cc, hh in dsts], mask, S.r1)
+             for half, mask, dsts in write1_plan(c, h)], local_sem=S.sent)
+        if (c, h) == (0, 0):
+            g.wait_ge(S.st, 16)
+        else:
+            g.sync.wait_ge(S.f0, 8)
+            g.sync.dma_start(T.y[0:64, :], buf[FIN]).then_inc(S.st, 16)
+            g.scalar.wait_ge(S.f1, 8)
+            g.scalar.dma_start(T.y[64:128, :], buf[FIN + 1]).then_inc(S.st, 16)
+            g.wait_ge(S.st, 32)
         g.wait_ge(S.sent, sent[0])
+        return
+
+    half = HALF_OF_HOST[h]
+    lo = h & 2
+    expect = 0
+    for cc in range(c + 1):
+        for hh in (lo, lo + 1):
+            for _, mask, dsts in write1_plan(cc, hh):
+                if (c, h) in dsts:
+                    expect += bits(mask)
+    g.wait_ge(S.r1, expect)
+    n_out = 2 * c + 2 if h < 2 else 2 * c
+    if n_out:
+        g.remote_dma_fused([transfer(list(range(n_out)), CB, [world(c, h ^ 3, COLLECTOR)], OFF8, S.r2)], local_sem=S.sent)
+    cable = [CB] if (h >= 2 or c) else []
+    if cable:
+        g.wait_ge(S.r2, 8)
+    fin = []
+    for j in (0, 1):
+        if (c, lo + j) == (0, 0):
+            continue
+        fin.append(transfer(list(range(2 * c + 1 + j)) + cable, FIN + half, [world(c, lo + j, 7)],
+                            ON8 if lo + j == h else OFF8, S["f%d" % half]))
+    g.remote_dma_fused(fin, local_sem=S.sent)
+    g.wait_ge(S.sent, sent[0])

from concourse.bass import DstId, RemoteDMATransfer

COLLECTOR = 3
HALF_OF_HOST = (0, 1, 1, 0)
SCRATCH = {"buf": ("dram", [9, 128, 128], "float32")}
XS, FIN, CB = 0, 2, 8
SEMAPHORES = ["ld", "r1", "r2", "f0", "f1", "st", "sent"]
LO4, HI4, OFF8, ON8 = 0x000F, 0x00F0, 0x00FF, 0xFF00


def bits(m):
    return sum((m >> i) & 1 for i in range(16))


def world(c, h, k):
    return 128 * h + 8 * c + k


def write1_plan(c, h):
    plan = []
    for hh in (h & 2, (h & 2) + 1):
        k = HALF_OF_HOST[hh]
        far = [(cc, hh) for cc in range(c, 4) if (cc, hh) != (c, h)]
        if hh == h:
            plan.append((k, ON8, [(c, h)]))
            if far:
                plan.append((k, LO4, far))
        else:
            plan.append((k, HI4 if c < 3 else OFF8, far))
    return plan


def rank_program(g, core, T, topo):
    S = T.sem
    buf = T.buf
    h, c, k = topo.host(core), topo.chip(core), core % 8
    if c > 3 or k not in (7, COLLECTOR):
        return
    sent = [0]

    def transfer(srcs, slot, dsts, mask, sem):
        ids = []
        for d in dsts:
            rid, pid = topo.addr(d, core)
            ids.append(DstId(rid=rid, pnc=pid))
        sent[0] += bits(mask)
        return RemoteDMATransfer(dst_ids=ids, dma_engine_mask=mask, remote_sem=sem, srcs=[buf[s] for s in srcs],
                                 dsts=[buf[slot] for _ in dsts], alu_op=1 if len(srcs) > 1 else 0)

    if k == 7:
        g.sync.dma_start(buf[XS:XS + 2], T.x[:]).then_inc(S.ld, 16)
        if (c, h) == (0, 0):
            g.scalar.dma_start(T.y[:], T.x[:]).then_inc(S.st, 16)
        g.wait_ge(S.ld, 16)
        slot = 2 * c + h % 2
        g.remote_dma_fused(
            [transfer([XS + half], slot, [world(cc, hh, COLLECTOR) for cc, hh in dsts], mask, S.r1)
             for half, mask, dsts in write1_plan(c, h)], local_sem=S.sent)
        if (c, h) == (0, 0):
            g.wait_ge(S.st, 16)
        else:
            g.sync.wait_ge(S.f0, 8)
            g.sync.dma_start(T.y[0:64, :], buf[FIN]).then_inc(S.st, 16)
            g.scalar.wait_ge(S.f1, 8)
            g.scalar.dma_start(T.y[64:128, :], buf[FIN + 1]).then_inc(S.st, 16)
            g.wait_ge(S.st, 32)
        g.wait_ge(S.sent, sent[0])
        return

    half = HALF_OF_HOST[h]
    lo = h & 2
    expect = 0
    for cc in range(c + 1):
        for hh in (lo, lo + 1):
            for _, mask, dsts in write1_plan(cc, hh):
                if (c, h) in dsts:
                    expect += bits(mask)
    g.wait_ge(S.r1, expect)
    n_out = 2 * c + 2 if h < 2 else 2 * c
    if n_out:
        g.remote_dma_fused([transfer(list(range(n_out)), CB, [world(c, h ^ 3, COLLECTOR)], OFF8, S.r2)], local_sem=S.sent)
    cable = [CB] if (h >= 2 or c) else []
    if cable:
        g.wait_ge(S.r2, 8)
    fin = []
    for j in (0, 1):
        if (c, lo + j) == (0, 0):
            continue
        fin.append(transfer(list(range(2 * c + 1 + j)) + cable, FIN + half, [world(c, lo + j, 7)],
                            ON8 if lo + j == h else OFF8, S["f%d" % half]))
    g.remote_dma_fused(fin, local_sem=S.sent)
    g.wait_ge(S.sent, sent[0])
